import numpy as np, ml_dtypes
CORES = [22,38,54,62,70,110,23,39,55,63,71,111]
N = 12
F = 64
GROUPS = [[0,1,4,6,7,8],[2,3,5,9,10,11]]
def setup_inputs(rng):
    return {"x": rng.standard_normal((N, 128, F), dtype=np.float32).astype(ml_dtypes.bfloat16), "w": (rng.standard_normal((N, 128, 128), dtype=np.float32) / 11).astype(ml_dtypes.bfloat16)}
def setup_inputs_big(rng):
    d = setup_inputs(rng)
    for k in ("x", "w"): d[k] = (d[k].astype(np.float32) * 1024.0).astype(d[k].dtype)
    return d
def setup_inputs_small(rng):
    d = setup_inputs(rng)
    for k in ("x", "w"): d[k] = (d[k].astype(np.float32) * (1 / 1024.0)).astype(d[k].dtype)
    return d
def setup_inputs_apart(rng):
    d = setup_inputs(rng)
    f = (10.0 ** rng.permutation(np.linspace(-1.5, 1.5, N))).astype(np.float32).reshape(N, 1, 1)
    for k in ("x", "w"): d[k] = (d[k].astype(np.float32) * f).astype(d[k].dtype)
    return d
def reference(x, w):
    X, W = x.astype(np.float64), w.astype(np.float64)
    s = sum(W[g[0]].T @ np.maximum(sum(X[j] for j in g), 0.0) for g in GROUPS).astype(ml_dtypes.bfloat16)
    return {"y": np.broadcast_to(s, (N,) + s.shape)}

@@ -1,0 +1,194 @@
+from concourse.bass import DstId, RemoteDMATransfer
+from concourse.mybir import AluOpType
+
+N = 12
+F = 64
+M = 128
+NG = 2
+NREP = 3
+E1 = 8
+E2 = 8
+
+SCRATCH = {
+    "xw": ("sbuf", [128, F + M], "bfloat16"),
+    "lx": ("sbuf", [128, N * F], "bfloat16"),
+    "lw": ("sbuf", [128, NG * (F + M)], "bfloat16"),
+    "zero": ("sbuf", [128, F], "bfloat16"),
+    "t0": ("sbuf", [128, F], "bfloat16"),
+    "t1": ("sbuf", [128, F], "bfloat16"),
+    "ys": ("sbuf", [128, F], "bfloat16"),
+    "yl": ("sbuf", [128, F], "bfloat16"),
+    "acc0": ("psum", [128, 512], "float32"),
+    "acc1": ("psum", [128, 512], "float32"),
+    "yp": ("psum", [128, 512], "float32"),
+}
+SEMAPHORES = ["ldx", "ldw", "zs", "v0", "v1", "ms", "yready", "sent", "yarr", "st"] + ["a%d" % j for j in range(N)]
+
+
+def _plan(T, topo):
+    cores = list(T.cores)
+    groups = T.tables["GROUPS"]
+    n = len(cores)
+    chip = [topo.chip(c) for c in cores]
+    heads = [grp[0] for grp in groups]
+    reps = list(heads)
+    while len(reps) < NREP:
+        best = None
+        for r in range(n):
+            if r in reps:
+                continue
+            key = (sum(1 for q in reps if chip[q] == chip[r]),
+                   -sum(1 for q in reps if topo.mates(chip[q], chip[r])),
+                   sum(1 for q in reps if topo.same_plane(chip[q], chip[r])), r)
+            if best is None or key < best:
+                best = key
+        reps.append(best[3])
+    rest = [r for r in range(n) if r not in reps]
+    serve = {q: [] for q in reps}
+    cap = -(-len(rest) // len(reps))
+    home = [r for r in rest if any(chip[q] == chip[r] for q in reps)]
+    for r in home + [r for r in rest if r not in home]:
+        best = None
+        for q in reps:
+            if len(serve[q]) >= cap or not topo.may_write(cores[q], cores[r]):
+                continue
+            key = (chip[q] != chip[r], not topo.same_plane(chip[q], chip[r]), len(serve[q]), q)
+            if best is None or key < best:
+                best = key
+        serve[best[3]].append(r)
+    dests, turn = [], 0
+    for i in range(n):
+        if i in reps:
+            p = reps.index(i)
+            dests.append(reps[p + 1:] + reps[:p])
+        else:
+            p = turn % len(reps)
+            turn += 1
+            dests.append(reps[p:] + reps[:p])
+    return heads, reps, serve, dests
+
+
+def _engines(topo, src, dsts, count, avoid=0):
+    m = ~avoid
+    for d in dsts:
+        m &= topo.mask(src, d)
+    out, bit = 0, 1
+    while count and bit <= m:
+        if m & bit:
+            out |= bit
+            count -= 1
+        bit <<= 1
+    return out
+
+
+def _ids(topo, dsts):
+    return [DstId(rid=topo.addr(d)[0], pnc=topo.addr(d)[1]) for d in dsts]
+
+
+def rank_program(g, core, T, topo):
+    me = T.rank_of(core)
+    if me is None:
+        return
+    S = T.sem
+    cores = list(T.cores)
+    groups = T.tables["GROUPS"]
+    heads, reps, serve, dests = _plan(T, topo)
+    head_of = heads.index(me) if me in heads else None
+    sent = 0
+
+    g.sync.dma_start(T.xw[:, 0:F], T.x[:, :]).then_inc(S.ldx, 16)
+    if head_of is not None:
+        g.scalar.dma_start(T.xw[:, F:F + M], T.w[:, :]).then_inc(S.ldw, 16)
+
+    if dests[me]:
+        to = [cores[q] for q in dests[me]]
+        if head_of is None:
+            src, dst = T.xw[:, 0:F], T.lx[:, me * F:(me + 1) * F]
+        else:
+            src, dst = T.xw[:, 0:F + M], T.lw[:, head_of * (F + M):(head_of + 1) * (F + M)]
+        g.wait_ge(S.ldx, 16)
+        if head_of is not None:
+            g.wait_ge(S.ldw, 16)
+        g.remote_dma_fused([RemoteDMATransfer(dst_ids=_ids(topo, to), dma_engine_mask=_engines(topo, core, to, E1),
+                                              remote_sem=S["a%d" % me], srcs=[src], dsts=[dst] * len(to), alu_op=0)],
+                           local_sem=S.sent)
+        sent += E1
+
+    if me not in reps:
+        g.sync.wait_ge(S.yarr, E2)
+        g.sync.dma_start(T.y[:, :], T.yl[:, :]).then_inc(S.st, 16)
+        g.sync.wait_ge(S.st, 16)
+        g.wait_ge(S.sent, sent)
+        return
+
+    def x_of(j):
+        if j == me:
+            return T.xw[:, 0:F]
+        if j in heads:
+            k = heads.index(j) * (F + M)
+            return T.lw[:, k:k + F]
+        return T.lx[:, j * F:(j + 1) * F]
+
+    def w_of(k):
+        if heads[k] == me:
+            return T.xw[:, F:F + M]
+        return T.lw[:, k * (F + M) + F:(k + 1) * (F + M)]
+
+    def here(queue, j):
+        if j == me:
+            queue.wait_ge(S.ldx, 16)
+        else:
+            queue.wait_ge(S["a%d" % j], E1)
+
+    v = g.vector
+    acc = [T.acc0[:, 0:F], T.acc1[:, 0:F]]
+    tt = [T.t0[:, :], T.t1[:, :]]
+    vs = [S.v0, S.v1]
+    order = sorted(range(len(cores)), key=lambda j: (-1 if j == me else dests[j].index(me), j))
+    v.memset(T.zero[:, :], 0.0).then_inc(S.zs, 1)
+    v.wait_ge(S.zs, 1)
+    first = [None] * len(groups)
+    done = [0] * len(groups)
+    finish = []
+    for j in order:
+        k = [gi for gi, grp in enumerate(groups) if j in grp][0]
+        here(v, j)
+        if first[k] is None:
+            first[k] = x_of(j)
+            continue
+        if done[k] == 0:
+            v.tensor_tensor(acc[k], first[k], x_of(j), AluOpType.add).then_inc(vs[k], 1)
+        else:
+            v.wait_ge(vs[k], done[k])
+            v.tensor_tensor(acc[k], acc[k], x_of(j), AluOpType.add).then_inc(vs[k], 1)
+        done[k] += 1
+        if done[k] == len(groups[k]) - 1:
+            v.wait_ge(vs[k], done[k])
+            v.tensor_tensor(tt[k], acc[k], T.zero[:, :], AluOpType.max).then_inc(vs[k], 1)
+            done[k] += 1
+            finish.append(k)
+
+    te = g.tensor
+    for n_, k in enumerate(finish):
+        if heads[k] == me:
+            te.wait_ge(S.ldw, 16)
+        else:
+            here(te, heads[k])
+        te.wait_ge(vs[k], done[k])
+        mm = te.matmul(T.yp[:, 0:F], w_of(k), tt[k], n_ == 0, n_ == len(finish) - 1)
+    mm.then_inc(S.ms, 1)
+    v.wait_ge(S.ms, 1)
+    v.tensor_copy(T.ys[:, :], T.yp[:, 0:F]).then_inc(S.yready, 1)
+
+    if serve[me]:
+        to = [cores[r] for r in serve[me]]
+        g.wait_ge(S.yready, 1)
+        g.remote_dma_fused([RemoteDMATransfer(dst_ids=_ids(topo, to), dma_engine_mask=_engines(topo, core, to, E2),
+                                              remote_sem=S.yarr, srcs=[T.ys[:, :]], dsts=[T.yl[:, :]] * len(to),
+                                              alu_op=0)], local_sem=S.sent)
+        sent += E2
+    g.sync.wait_ge(S.yready, 1)
+    g.sync.dma_start(T.y[:, :], T.ys[:, :]).then_inc(S.st, 16)
+    g.sync.wait_ge(S.st, 16)
+    if sent:
+        g.wait_ge(S.sent, sent)

@@ -11,13 +11,14 @@ E2 = 8
 
 SCRATCH = {
     "xw": ("sbuf", [128, F + M], "bfloat16"),
+    "xd": ("dram", [128, F], "bfloat16"),
     "lx": ("sbuf", [128, N * F], "bfloat16"),
     "lw": ("sbuf", [128, NG * (F + M)], "bfloat16"),
     "zero": ("sbuf", [128, F], "bfloat16"),
     "t0": ("sbuf", [128, F], "bfloat16"),
     "t1": ("sbuf", [128, F], "bfloat16"),
     "ys": ("sbuf", [128, F], "bfloat16"),
-    "yl": ("sbuf", [128, F], "bfloat16"),
+    "yl": ("dram", [128, F], "bfloat16"),
     "acc0": ("psum", [128, 512], "float32"),
     "acc1": ("psum", [128, 512], "float32"),
     "yp": ("psum", [128, 512], "float32"),
@@ -68,8 +69,8 @@ def _plan(T, topo):
     return heads, reps, serve, dests
 
 
-def _engines(topo, src, dsts, count, avoid=0):
-    m = ~avoid
+def _engines(topo, src, dsts, count):
+    m = -1
     for d in dsts:
         m &= topo.mask(src, d)
     out, bit = 0, 1
@@ -96,14 +97,15 @@ def rank_program(g, core, T, topo):
     head_of = heads.index(me) if me in heads else None
     sent = 0
 
-    g.sync.dma_start(T.xw[:, 0:F], T.x[:, :]).then_inc(S.ldx, 16)
+    mine = T.xw[:, 0:F] if me in reps else T.xd[:, :]
+    g.sync.dma_start(mine, T.x[:, :]).then_inc(S.ldx, 16)
     if head_of is not None:
         g.scalar.dma_start(T.xw[:, F:F + M], T.w[:, :]).then_inc(S.ldw, 16)
 
     if dests[me]:
         to = [cores[q] for q in dests[me]]
         if head_of is None:
-            src, dst = T.xw[:, 0:F], T.lx[:, me * F:(me + 1) * F]
+            src, dst = mine, T.lx[:, me * F:(me + 1) * F]
         else:
             src, dst = T.xw[:, 0:F + M], T.lw[:, head_of * (F + M):(head_of + 1) * (F + M)]
         g.wait_ge(S.ldx, 16)
@@ -140,11 +142,16 @@ def rank_program(g, core, T, topo):
         else:
             queue.wait_ge(S["a%d" % j], E1)
 
+    def expected(j):
+        if j == me:
+            return 0
+        return (dests[j].index(me) + 1) * (F + M if j in heads else F)
+
     v = g.vector
     acc = [T.acc0[:, 0:F], T.acc1[:, 0:F]]
     tt = [T.t0[:, :], T.t1[:, :]]
     vs = [S.v0, S.v1]
-    order = sorted(range(len(cores)), key=lambda j: (-1 if j == me else dests[j].index(me), j))
+    order = sorted(range(len(cores)), key=lambda j: (expected(j), j in heads, j))
     v.memset(T.zero[:, :], 0.0).then_inc(S.zs, 1)
     v.wait_ge(S.zs, 1)
     first = [None] * len(groups)

@@ -15,6 +15,9 @@ SCRATCH = {
     "lx": ("sbuf", [128, N * F], "bfloat16"),
     "lw": ("sbuf", [128, NG * (F + M)], "bfloat16"),
     "zero": ("sbuf", [128, F], "bfloat16"),
+    "idsrc": ("sbuf", [128, 129], "bfloat16"),
+    "idd": ("dram", [129, 128], "bfloat16"),
+    "ident": ("sbuf", [128, 128], "bfloat16"),
     "t0": ("sbuf", [128, F], "bfloat16"),
     "t1": ("sbuf", [128, F], "bfloat16"),
     "ys": ("sbuf", [128, F], "bfloat16"),
@@ -23,7 +26,8 @@ SCRATCH = {
     "acc1": ("psum", [128, 512], "float32"),
     "yp": ("psum", [128, 512], "float32"),
 }
-SEMAPHORES = ["ldx", "ldw", "zs", "v0", "v1", "ms", "yready", "sent", "yarr", "st"] + ["a%d" % j for j in range(N)]
+SEMAPHORES = (["ldx", "ldw", "zs", "zz", "ida", "idb", "v0", "v1", "r0", "r1", "ms", "yready", "sent", "yarr", "st"]
+              + ["a%d" % j for j in range(N)])
 
 
 def _plan(T, topo):
@@ -44,33 +48,39 @@ def _plan(T, topo):
             if best is None or key < best:
                 best = key
         reps.append(best[3])
-    rest = [r for r in range(n) if r not in reps]
     serve = {q: [] for q in reps}
-    cap = -(-len(rest) // len(reps))
-    home = [r for r in rest if any(chip[q] == chip[r] for q in reps)]
-    for r in home + [r for r in rest if r not in home]:
+    away = []
+    for r in range(n):
+        if r in reps:
+            continue
+        at_home = [q for q in reps if chip[q] == chip[r]]
+        if at_home:
+            serve[at_home[0]].append(r)
+        else:
+            away.append(r)
+    load = {q: 0 for q in heads}
+    for r in away:
         best = None
-        for q in reps:
-            if len(serve[q]) >= cap or not topo.may_write(cores[q], cores[r]):
-                continue
-            key = (chip[q] != chip[r], not topo.same_plane(chip[q], chip[r]), len(serve[q]), q)
-            if best is None or key < best:
-                best = key
-        serve[best[3]].append(r)
+        for q in heads:
+            if topo.may_write(cores[q], cores[r]):
+                key = (load[q], not topo.same_plane(chip[q], chip[r]), q)
+                if best is None or key < best:
+                    best = key
+        serve[best[2]].append(r)
+        load[best[2]] += 1
+    others = [q for q in reps if q not in heads]
     dests, turn = [], 0
     for i in range(n):
-        if i in reps:
-            p = reps.index(i)
-            dests.append(reps[p + 1:] + reps[:p])
-        else:
-            p = turn % len(reps)
+        p = turn % len(heads)
+        if i not in heads:
             turn += 1
-            dests.append(reps[p:] + reps[:p])
+        d = heads[p:] + heads[:p] + others
+        dests.append([q for q in d if q != i])
     return heads, reps, serve, dests
 
 
-def _engines(topo, src, dsts, count):
-    m = -1
+def _engines(topo, src, dsts, count, avoid=0):
+    m = ~avoid
     for d in dsts:
         m &= topo.mask(src, d)
     out, bit = 0, 1
@@ -147,53 +157,61 @@ def rank_program(g, core, T, topo):
             return 0
         return (dests[j].index(me) + 1) * (F + M if j in heads else F)
 
-    v = g.vector
+    v, te = g.vector, g.tensor
     acc = [T.acc0[:, 0:F], T.acc1[:, 0:F]]
     tt = [T.t0[:, :], T.t1[:, :]]
     vs = [S.v0, S.v1]
-    order = sorted(range(len(cores)), key=lambda j: (expected(j), j in heads, j))
-    v.memset(T.zero[:, :], 0.0).then_inc(S.zs, 1)
+    rs = [S.r0, S.r1]
+
+    v.memset(T.idsrc[:, :], 0.0).then_inc(S.zs, 1)
     v.wait_ge(S.zs, 1)
-    first = [None] * len(groups)
-    done = [0] * len(groups)
+    v.memset(T.idsrc[:, 0:1], 1.0).then_inc(S.zs, 1)
+    v.memset(T.zero[:, :], 0.0).then_inc(S.zz, 1)
+    g.scalar.wait_ge(S.zs, 2)
+    g.scalar.dma_start(T.idd[:, :], T.idsrc[:, :]).then_inc(S.ida, 16)
+    g.scalar.wait_ge(S.ida, 16)
+    g.scalar.dma_start(T.ident[:, :], T.idd[0:128, :]).then_inc(S.idb, 16)
+
+    order = sorted(range(len(cores)), key=lambda j: (expected(j), j in heads, j))
+    seen = [0] * len(groups)
     finish = []
+    te.wait_ge(S.idb, 16)
     for j in order:
         k = [gi for gi, grp in enumerate(groups) if j in grp][0]
-        here(v, j)
-        if first[k] is None:
-            first[k] = x_of(j)
-            continue
-        if done[k] == 0:
-            v.tensor_tensor(acc[k], first[k], x_of(j), AluOpType.add).then_inc(vs[k], 1)
-        else:
-            v.wait_ge(vs[k], done[k])
-            v.tensor_tensor(acc[k], acc[k], x_of(j), AluOpType.add).then_inc(vs[k], 1)
-        done[k] += 1
-        if done[k] == len(groups[k]) - 1:
-            v.wait_ge(vs[k], done[k])
-            v.tensor_tensor(tt[k], acc[k], T.zero[:, :], AluOpType.max).then_inc(vs[k], 1)
-            done[k] += 1
+        here(te, j)
+        seen[k] += 1
+        last = seen[k] == len(groups[k])
+        mm = te.matmul(acc[k], T.ident[:, :], x_of(j), seen[k] == 1, last)
+        if last:
+            mm.then_inc(vs[k], 1)
             finish.append(k)
 
-    te = g.tensor
+    v.wait_ge(S.zz, 1)
     for n_, k in enumerate(finish):
+        v.wait_ge(vs[k], 1)
+        v.tensor_tensor(tt[k], acc[k], T.zero[:, :], AluOpType.max).then_inc(rs[k], 1)
         if heads[k] == me:
             te.wait_ge(S.ldw, 16)
-        else:
-            here(te, heads[k])
-        te.wait_ge(vs[k], done[k])
+        te.wait_ge(rs[k], 1)
         mm = te.matmul(T.yp[:, 0:F], w_of(k), tt[k], n_ == 0, n_ == len(finish) - 1)
     mm.then_inc(S.ms, 1)
     v.wait_ge(S.ms, 1)
     v.tensor_copy(T.ys[:, :], T.yp[:, 0:F]).then_inc(S.yready, 1)
 
-    if serve[me]:
-        to = [cores[r] for r in serve[me]]
+    to = [cores[r] for r in serve[me]]
+    far = [d for d in to if topo.chip(d) != topo.chip(core)]
+    near = [d for d in to if d not in far]
+    busy = 0
+    if to:
         g.wait_ge(S.yready, 1)
-        g.remote_dma_fused([RemoteDMATransfer(dst_ids=_ids(topo, to), dma_engine_mask=_engines(topo, core, to, E2),
-                                              remote_sem=S.yarr, srcs=[T.ys[:, :]], dsts=[T.yl[:, :]] * len(to),
-                                              alu_op=0)], local_sem=S.sent)
-        sent += E2
+    for part in (far, near):
+        if part:
+            em = _engines(topo, core, part, E2, busy)
+            busy |= em
+            g.remote_dma_fused([RemoteDMATransfer(dst_ids=_ids(topo, part), dma_engine_mask=em, remote_sem=S.yarr,
+                                                  srcs=[T.ys[:, :]], dsts=[T.yl[:, :]] * len(part), alu_op=0)],
+                               local_sem=S.sent)
+            sent += E2
     g.sync.wait_ge(S.yready, 1)
     g.sync.dma_start(T.y[:, :], T.ys[:, :]).then_inc(S.st, 16)
     g.sync.wait_ge(S.st, 16)

@@ -5,29 +5,33 @@ N = 12
 F = 64
 M = 128
 NG = 2
-NREP = 3
-E1 = 8
-E2 = 8
+E = 8
+SHARE = (3, 2, 1)
 
 SCRATCH = {
-    "xw": ("sbuf", [128, F + M], "bfloat16"),
+    "xs": ("sbuf", [128, F], "bfloat16"),
+    "ws": ("sbuf", [128, M], "bfloat16"),
     "xd": ("dram", [128, F], "bfloat16"),
     "lx": ("sbuf", [128, N * F], "bfloat16"),
-    "lw": ("sbuf", [128, NG * (F + M)], "bfloat16"),
+    "lw": ("sbuf", [128, M], "bfloat16"),
     "zero": ("sbuf", [128, F], "bfloat16"),
-    "idsrc": ("sbuf", [128, 129], "bfloat16"),
-    "idd": ("dram", [129, 128], "bfloat16"),
+    "ones": ("sbuf", [128, 128], "bfloat16"),
     "ident": ("sbuf", [128, 128], "bfloat16"),
-    "t0": ("sbuf", [128, F], "bfloat16"),
-    "t1": ("sbuf", [128, F], "bfloat16"),
+    "t": ("sbuf", [128, F], "bfloat16"),
+    "ps": ("sbuf", [128, F], "bfloat16"),
+    "lp": ("sbuf", [128, NG * F], "bfloat16"),
     "ys": ("sbuf", [128, F], "bfloat16"),
-    "yl": ("dram", [128, F], "bfloat16"),
-    "acc0": ("psum", [128, 512], "float32"),
-    "acc1": ("psum", [128, 512], "float32"),
+    "acc": ("psum", [128, 512], "float32"),
     "yp": ("psum", [128, 512], "float32"),
 }
-SEMAPHORES = (["ldx", "ldw", "zs", "zz", "ida", "idb", "v0", "v1", "r0", "r1", "ms", "yready", "sent", "yarr", "st"]
-              + ["a%d" % j for j in range(N)])
+SEMAPHORES = (["ldx", "ldw", "zs", "zz", "idb", "vs", "rs", "ms", "pready", "yready", "sent", "wa", "st"]
+              + ["pa%d" % k for k in range(NG)] + ["a%d" % j for j in range(N)])
+
+
+def _hops(topo, a, b):
+    if a == b:
+        return 0
+    return 1 if topo.mates(a, b) or topo.same_plane(a, b) else 2
 
 
 def _plan(T, topo):
@@ -36,47 +40,37 @@ def _plan(T, topo):
     n = len(cores)
     chip = [topo.chip(c) for c in cores]
     heads = [grp[0] for grp in groups]
-    reps = list(heads)
-    while len(reps) < NREP:
-        best = None
-        for r in range(n):
-            if r in reps:
-                continue
-            key = (sum(1 for q in reps if chip[q] == chip[r]),
-                   -sum(1 for q in reps if topo.mates(chip[q], chip[r])),
-                   sum(1 for q in reps if topo.same_plane(chip[q], chip[r])), r)
-            if best is None or key < best:
-                best = key
-        reps.append(best[3])
-    serve = {q: [] for q in reps}
-    away = []
-    for r in range(n):
-        if r in reps:
-            continue
-        at_home = [q for q in reps if chip[q] == chip[r]]
-        if at_home:
-            serve[at_home[0]].append(r)
-        else:
-            away.append(r)
-    load = {q: 0 for q in heads}
-    for r in away:
-        best = None
-        for q in heads:
-            if topo.may_write(cores[q], cores[r]):
-                key = (load[q], not topo.same_plane(chip[q], chip[r]), q)
-                if best is None or key < best:
-                    best = key
-        serve[best[2]].append(r)
-        load[best[2]] += 1
-    others = [q for q in reps if q not in heads]
-    dests, turn = [], 0
-    for i in range(n):
-        p = turn % len(heads)
-        if i not in heads:
-            turn += 1
-        d = heads[p:] + heads[:p] + others
-        dests.append([q for q in d if q != i])
-    return heads, reps, serve, dests
+    chips = sorted(set(chip))
+    per = len(chips) // len(groups)
+
+    def members(c, k):
+        return sum(1 for r in groups[k] if chip[r] == c)
+
+    owner = {chip[h]: k for k, h in enumerate(heads)}
+    rest = [c for c in chips if c not in owner]
+    rest.sort(key=lambda c: (-(max(members(c, k) for k in range(len(groups)))
+                               - min(members(c, k) for k in range(len(groups)))), c))
+    for c in rest:
+        free = [k for k in range(len(groups)) if sum(1 for o in owner.values() if o == k) < per]
+        owner[c] = max(free, key=lambda k: (members(c, k), -k))
+    reps, far, near = [], {}, {}
+    for k, grp in enumerate(groups):
+        hc = chip[heads[k]]
+        mine = sorted((c for c in chips if owner[c] == k), key=lambda c: (_hops(topo, hc, c), -members(c, k), c))
+        rk = []
+        for c in mine:
+            here = [r for r in range(n) if chip[r] == c]
+            pick = [r for r in here if r == heads[k]] or [r for r in here if r in grp] or here
+            rk.append(pick[0])
+        reps.append(rk)
+        away = sorted((r for r in range(n) if owner[chip[r]] != k), key=lambda r: (-_hops(topo, hc, chip[r]), r))
+        at = 0
+        for i, q in enumerate(rk):
+            part = away[at:at + SHARE[i]]
+            at += SHARE[i]
+            far[q] = sorted(part, key=lambda r: (-_hops(topo, chip[q], chip[r]), r))
+            near[q] = [r for r in range(n) if chip[r] == chip[q] and r != q]
+    return heads, reps, far, near
 
 
 def _engines(topo, src, dsts, count, avoid=0):
@@ -103,117 +97,90 @@ def rank_program(g, core, T, topo):
     S = T.sem
     cores = list(T.cores)
     groups = T.tables["GROUPS"]
-    heads, reps, serve, dests = _plan(T, topo)
-    head_of = heads.index(me) if me in heads else None
+    heads, reps, far, near = _plan(T, topo)
+    grp_of = [[k for k, grp in enumerate(groups) if j in grp][0] for j in range(len(cores))]
+    dests = [[q for q in reps[grp_of[j]] if q != j] for j in range(len(cores))]
+    job = [k for k in range(len(groups)) if me in reps[k]]
+    is_head = me in heads
+    v, te = g.vector, g.tensor
     sent = 0
 
-    mine = T.xw[:, 0:F] if me in reps else T.xd[:, :]
+    def write(src, dst, to, sem, avoid=0):
+        em = _engines(topo, core, to, E, avoid)
+        g.remote_dma_fused([RemoteDMATransfer(dst_ids=_ids(topo, to), dma_engine_mask=em, remote_sem=sem,
+                                              srcs=[src], dsts=[dst] * len(to), alu_op=0)], local_sem=S.sent)
+        return em
+
+    mine = T.xs[:, :] if job else T.xd[:, :]
     g.sync.dma_start(mine, T.x[:, :]).then_inc(S.ldx, 16)
-    if head_of is not None:
-        g.scalar.dma_start(T.xw[:, F:F + M], T.w[:, :]).then_inc(S.ldw, 16)
+    if is_head:
+        g.scalar.dma_start(T.ws[:, :], T.w[:, :]).then_inc(S.ldw, 16)
+    if job:
+        v.memset(T.ones[:, :], 1.0).then_inc(S.zs, 1)
+        v.memset(T.zero[:, :], 0.0).then_inc(S.zz, 1)
 
-    if dests[me]:
-        to = [cores[q] for q in dests[me]]
-        if head_of is None:
-            src, dst = mine, T.lx[:, me * F:(me + 1) * F]
-        else:
-            src, dst = T.xw[:, 0:F + M], T.lw[:, head_of * (F + M):(head_of + 1) * (F + M)]
-        g.wait_ge(S.ldx, 16)
-        if head_of is not None:
-            g.wait_ge(S.ldw, 16)
-        g.remote_dma_fused([RemoteDMATransfer(dst_ids=_ids(topo, to), dma_engine_mask=_engines(topo, core, to, E1),
-                                              remote_sem=S["a%d" % me], srcs=[src], dsts=[dst] * len(to), alu_op=0)],
-                           local_sem=S.sent)
-        sent += E1
+    to = [cores[q] for q in dests[me]]
+    g.wait_ge(S.ldx, 16)
+    write(mine, T.lx[:, me * F:(me + 1) * F], to, S["a%d" % me])
+    sent += E
+    if is_head:
+        g.wait_ge(S.ldw, 16)
+        write(T.ws[:, :], T.lw[:, :], to, S.wa)
+        sent += E
 
-    if me not in reps:
-        g.sync.wait_ge(S.yarr, E2)
-        g.sync.dma_start(T.y[:, :], T.yl[:, :]).then_inc(S.st, 16)
+    if not job:
+        for k in range(len(groups)):
+            v.wait_ge(S["pa%d" % k], E)
+        v.tensor_tensor(T.ys[:, :], T.lp[:, 0:F], T.lp[:, F:2 * F], AluOpType.add).then_inc(S.yready, 1)
+        g.sync.wait_ge(S.yready, 1)
+        g.sync.dma_start(T.y[:, :], T.ys[:, :]).then_inc(S.st, 16)
         g.sync.wait_ge(S.st, 16)
         g.wait_ge(S.sent, sent)
         return
 
-    def x_of(j):
-        if j == me:
-            return T.xw[:, 0:F]
-        if j in heads:
-            k = heads.index(j) * (F + M)
-            return T.lw[:, k:k + F]
-        return T.lx[:, j * F:(j + 1) * F]
+    k = job[0]
+    other = 1 - k
+    g.wait_ge(S.zs, 1)
+    g.affine_select(T.ident[:, :], T.ones[:, :], [[-1, 128]], AluOpType.is_equal, 0.0, 0, 1).then_inc(S.idb, 1)
 
-    def w_of(k):
-        if heads[k] == me:
-            return T.xw[:, F:F + M]
-        return T.lw[:, k * (F + M) + F:(k + 1) * (F + M)]
-
-    def here(queue, j):
+    order = sorted(groups[k], key=lambda j: (0 if j == me else dests[j].index(me) + 1,
+                                             _hops(topo, topo.chip(cores[j]), topo.chip(core)), j))
+    te.wait_ge(S.idb, 1)
+    for i, j in enumerate(order):
         if j == me:
-            queue.wait_ge(S.ldx, 16)
+            te.wait_ge(S.ldx, 16)
+            xj = T.xs[:, :]
         else:
-            queue.wait_ge(S["a%d" % j], E1)
-
-    def expected(j):
-        if j == me:
-            return 0
-        return (dests[j].index(me) + 1) * (F + M if j in heads else F)
-
-    v, te = g.vector, g.tensor
-    acc = [T.acc0[:, 0:F], T.acc1[:, 0:F]]
-    tt = [T.t0[:, :], T.t1[:, :]]
-    vs = [S.v0, S.v1]
-    rs = [S.r0, S.r1]
-
-    v.memset(T.idsrc[:, :], 0.0).then_inc(S.zs, 1)
-    v.wait_ge(S.zs, 1)
-    v.memset(T.idsrc[:, 0:1], 1.0).then_inc(S.zs, 1)
-    v.memset(T.zero[:, :], 0.0).then_inc(S.zz, 1)
-    g.scalar.wait_ge(S.zs, 2)
-    g.scalar.dma_start(T.idd[:, :], T.idsrc[:, :]).then_inc(S.ida, 16)
-    g.scalar.wait_ge(S.ida, 16)
-    g.scalar.dma_start(T.ident[:, :], T.idd[0:128, :]).then_inc(S.idb, 16)
-
-    order = sorted(range(len(cores)), key=lambda j: (expected(j), j in heads, j))
-    seen = [0] * len(groups)
-    finish = []
-    te.wait_ge(S.idb, 16)
-    for j in order:
-        k = [gi for gi, grp in enumerate(groups) if j in grp][0]
-        here(te, j)
-        seen[k] += 1
-        last = seen[k] == len(groups[k])
-        mm = te.matmul(acc[k], T.ident[:, :], x_of(j), seen[k] == 1, last)
-        if last:
-            mm.then_inc(vs[k], 1)
-            finish.append(k)
+            te.wait_ge(S["a%d" % j], E)
+            xj = T.lx[:, j * F:(j + 1) * F]
+        mm = te.matmul(T.acc[:, 0:F], T.ident[:, :], xj, i == 0, i == len(order) - 1)
+    mm.then_inc(S.vs, 1)
 
     v.wait_ge(S.zz, 1)
-    for n_, k in enumerate(finish):
-        v.wait_ge(vs[k], 1)
-        v.tensor_tensor(tt[k], acc[k], T.zero[:, :], AluOpType.max).then_inc(rs[k], 1)
-        if heads[k] == me:
-            te.wait_ge(S.ldw, 16)
-        te.wait_ge(rs[k], 1)
-        mm = te.matmul(T.yp[:, 0:F], w_of(k), tt[k], n_ == 0, n_ == len(finish) - 1)
-    mm.then_inc(S.ms, 1)
+    v.wait_ge(S.vs, 1)
+    v.tensor_tensor(T.t[:, :], T.acc[:, 0:F], T.zero[:, :], AluOpType.max).then_inc(S.rs, 1)
+    if is_head:
+        te.wait_ge(S.ldw, 16)
+        wk = T.ws[:, :]
+    else:
+        te.wait_ge(S.wa, E)
+        wk = T.lw[:, :]
+    te.wait_ge(S.rs, 1)
+    te.matmul(T.yp[:, 0:F], wk, T.t[:, :], True, True).then_inc(S.ms, 1)
     v.wait_ge(S.ms, 1)
-    v.tensor_copy(T.ys[:, :], T.yp[:, 0:F]).then_inc(S.yready, 1)
+    v.tensor_copy(T.ps[:, :], T.yp[:, 0:F]).then_inc(S.pready, 1)
 
-    to = [cores[r] for r in serve[me]]
-    far = [d for d in to if topo.chip(d) != topo.chip(core)]
-    near = [d for d in to if d not in far]
+    land = T.lp[:, k * F:(k + 1) * F]
     busy = 0
-    if to:
-        g.wait_ge(S.yready, 1)
-    for part in (far, near):
+    g.wait_ge(S.pready, 1)
+    for part in (far[me], near[me]):
         if part:
-            em = _engines(topo, core, part, E2, busy)
-            busy |= em
-            g.remote_dma_fused([RemoteDMATransfer(dst_ids=_ids(topo, part), dma_engine_mask=em, remote_sem=S.yarr,
-                                                  srcs=[T.ys[:, :]], dsts=[T.yl[:, :]] * len(part), alu_op=0)],
-                               local_sem=S.sent)
-            sent += E2
+            busy |= write(T.ps[:, :], land, [cores[r] for r in part], S["pa%d" % k], busy)
+            sent += E
+
+    v.wait_ge(S["pa%d" % other], E)
+    v.tensor_tensor(T.ys[:, :], T.yp[:, 0:F], T.lp[:, other * F:(other + 1) * F], AluOpType.add).then_inc(S.yready, 1)
     g.sync.wait_ge(S.yready, 1)
     g.sync.dma_start(T.y[:, :], T.ys[:, :]).then_inc(S.st, 16)
     g.sync.wait_ge(S.st, 16)
-    if sent:
-        g.wait_ge(S.sent, sent)
+    g.wait_ge(S.sent, sent)

from concourse.bass import DstId, RemoteDMATransfer
from concourse.mybir import AluOpType

N = 12
F = 64
M = 128
NG = 2
E = 8
SHARE = (3, 2, 1)

SCRATCH = {
    "xs": ("sbuf", [128, F], "bfloat16"),
    "ws": ("sbuf", [128, M], "bfloat16"),
    "xd": ("dram", [128, F], "bfloat16"),
    "lx": ("sbuf", [128, N * F], "bfloat16"),
    "lw": ("sbuf", [128, M], "bfloat16"),
    "zero": ("sbuf", [128, F], "bfloat16"),
    "ones": ("sbuf", [128, 128], "bfloat16"),
    "ident": ("sbuf", [128, 128], "bfloat16"),
    "t": ("sbuf", [128, F], "bfloat16"),
    "ps": ("sbuf", [128, F], "bfloat16"),
    "lp": ("sbuf", [128, NG * F], "bfloat16"),
    "ys": ("sbuf", [128, F], "bfloat16"),
    "acc": ("psum", [128, 512], "float32"),
    "yp": ("psum", [128, 512], "float32"),
}
SEMAPHORES = (["ldx", "ldw", "zs", "zz", "idb", "vs", "rs", "ms", "pready", "yready", "sent", "wa", "st"]
              + ["pa%d" % k for k in range(NG)] + ["a%d" % j for j in range(N)])


def _hops(topo, a, b):
    if a == b:
        return 0
    return 1 if topo.mates(a, b) or topo.same_plane(a, b) else 2


def _plan(T, topo):
    cores = list(T.cores)
    groups = T.tables["GROUPS"]
    n = len(cores)
    chip = [topo.chip(c) for c in cores]
    heads = [grp[0] for grp in groups]
    chips = sorted(set(chip))
    per = len(chips) // len(groups)

    def members(c, k):
        return sum(1 for r in groups[k] if chip[r] == c)

    owner = {chip[h]: k for k, h in enumerate(heads)}
    rest = [c for c in chips if c not in owner]
    rest.sort(key=lambda c: (-(max(members(c, k) for k in range(len(groups)))
                               - min(members(c, k) for k in range(len(groups)))), c))
    for c in rest:
        free = [k for k in range(len(groups)) if sum(1 for o in owner.values() if o == k) < per]
        owner[c] = max(free, key=lambda k: (members(c, k), -k))
    reps, far, near = [], {}, {}
    for k, grp in enumerate(groups):
        hc = chip[heads[k]]
        mine = sorted((c for c in chips if owner[c] == k), key=lambda c: (_hops(topo, hc, c), -members(c, k), c))
        rk = []
        for c in mine:
            here = [r for r in range(n) if chip[r] == c]
            pick = [r for r in here if r == heads[k]] or [r for r in here if r in grp] or here
            rk.append(pick[0])
        reps.append(rk)
        away = sorted((r for r in range(n) if owner[chip[r]] != k), key=lambda r: (-_hops(topo, hc, chip[r]), r))
        at = 0
        for i, q in enumerate(rk):
            part = away[at:at + SHARE[i]]
            at += SHARE[i]
            far[q] = sorted(part, key=lambda r: (-_hops(topo, chip[q], chip[r]), r))
            near[q] = [r for r in range(n) if chip[r] == chip[q] and r != q]
    return heads, reps, far, near


def _engines(topo, src, dsts, count, avoid=0):
    m = ~avoid
    for d in dsts:
        m &= topo.mask(src, d)
    out, bit = 0, 1
    while count and bit <= m:
        if m & bit:
            out |= bit
            count -= 1
        bit <<= 1
    return out


def _ids(topo, dsts):
    return [DstId(rid=topo.addr(d)[0], pnc=topo.addr(d)[1]) for d in dsts]


def rank_program(g, core, T, topo):
    me = T.rank_of(core)
    if me is None:
        return
    S = T.sem
    cores = list(T.cores)
    groups = T.tables["GROUPS"]
    heads, reps, far, near = _plan(T, topo)
    grp_of = [[k for k, grp in enumerate(groups) if j in grp][0] for j in range(len(cores))]
    dests = [[q for q in reps[grp_of[j]] if q != j] for j in range(len(cores))]
    job = [k for k in range(len(groups)) if me in reps[k]]
    is_head = me in heads
    v, te = g.vector, g.tensor
    sent = 0

    def write(src, dst, to, sem, avoid=0):
        em = _engines(topo, core, to, E, avoid)
        g.remote_dma_fused([RemoteDMATransfer(dst_ids=_ids(topo, to), dma_engine_mask=em, remote_sem=sem,
                                              srcs=[src], dsts=[dst] * len(to), alu_op=0)], local_sem=S.sent)
        return em

    mine = T.xs[:, :] if job else T.xd[:, :]
    g.sync.dma_start(mine, T.x[:, :]).then_inc(S.ldx, 16)
    if is_head:
        g.scalar.dma_start(T.ws[:, :], T.w[:, :]).then_inc(S.ldw, 16)
    if job:
        v.memset(T.ones[:, :], 1.0).then_inc(S.zs, 1)
        v.memset(T.zero[:, :], 0.0).then_inc(S.zz, 1)

    to = [cores[q] for q in dests[me]]
    g.wait_ge(S.ldx, 16)
    write(mine, T.lx[:, me * F:(me + 1) * F], to, S["a%d" % me])
    sent += E
    if is_head:
        g.wait_ge(S.ldw, 16)
        write(T.ws[:, :], T.lw[:, :], to, S.wa)
        sent += E

    if not job:
        for k in range(len(groups)):
            v.wait_ge(S["pa%d" % k], E)
        v.tensor_tensor(T.ys[:, :], T.lp[:, 0:F], T.lp[:, F:2 * F], AluOpType.add).then_inc(S.yready, 1)
        g.sync.wait_ge(S.yready, 1)
        g.sync.dma_start(T.y[:, :], T.ys[:, :]).then_inc(S.st, 16)
        g.sync.wait_ge(S.st, 16)
        g.wait_ge(S.sent, sent)
        return

    k = job[0]
    other = 1 - k
    g.wait_ge(S.zs, 1)
    g.affine_select(T.ident[:, :], T.ones[:, :], [[-1, 128]], AluOpType.is_equal, 0.0, 0, 1).then_inc(S.idb, 1)

    order = sorted(groups[k], key=lambda j: (0 if j == me else dests[j].index(me) + 1,
                                             _hops(topo, topo.chip(cores[j]), topo.chip(core)), j))
    te.wait_ge(S.idb, 1)
    for i, j in enumerate(order):
        if j == me:
            te.wait_ge(S.ldx, 16)
            xj = T.xs[:, :]
        else:
            te.wait_ge(S["a%d" % j], E)
            xj = T.lx[:, j * F:(j + 1) * F]
        mm = te.matmul(T.acc[:, 0:F], T.ident[:, :], xj, i == 0, i == len(order) - 1)
    mm.then_inc(S.vs, 1)

    v.wait_ge(S.zz, 1)
    v.wait_ge(S.vs, 1)
    v.tensor_tensor(T.t[:, :], T.acc[:, 0:F], T.zero[:, :], AluOpType.max).then_inc(S.rs, 1)
    if is_head:
        te.wait_ge(S.ldw, 16)
        wk = T.ws[:, :]
    else:
        te.wait_ge(S.wa, E)
        wk = T.lw[:, :]
    te.wait_ge(S.rs, 1)
    te.matmul(T.yp[:, 0:F], wk, T.t[:, :], True, True).then_inc(S.ms, 1)
    v.wait_ge(S.ms, 1)
    v.tensor_copy(T.ps[:, :], T.yp[:, 0:F]).then_inc(S.pready, 1)

    land = T.lp[:, k * F:(k + 1) * F]
    busy = 0
    g.wait_ge(S.pready, 1)
    for part in (far[me], near[me]):
        if part:
            busy |= write(T.ps[:, :], land, [cores[r] for r in part], S["pa%d" % k], busy)
            sent += E

    v.wait_ge(S["pa%d" % other], E)
    v.tensor_tensor(T.ys[:, :], T.yp[:, 0:F], T.lp[:, other * F:(other + 1) * F], AluOpType.add).then_inc(S.yready, 1)
    g.sync.wait_ge(S.yready, 1)
    g.sync.dma_start(T.y[:, :], T.ys[:, :]).then_inc(S.st, 16)
    g.sync.wait_ge(S.st, 16)
    g.wait_ge(S.sent, sent)
